import numpy as np
import ml_dtypes


def mxq(x, axis, fmt="e4m3"):
    dtype, down = {"e4m3": (ml_dtypes.float8_e4m3fn, 7), "e5m2": (ml_dtypes.float8_e5m2, 14)}[fmt]
    v = np.moveaxis(np.asarray(x, np.float32).astype(ml_dtypes.bfloat16).astype(np.float64), axis, -1)
    blocks = v.reshape(v.shape[:-1] + (-1, 32))
    amax = np.abs(blocks).max(-1, keepdims=True)
    byte = np.maximum(np.where(amax > 0, np.frexp(amax)[1] - 1 + 127, 0) - down, 1)
    scale = np.exp2(byte - 127.0)
    codes = (blocks / scale).astype(np.float32).astype(dtype).astype(np.float64)
    return np.moveaxis((codes * scale).reshape(v.shape), -1, axis)


WIDE = False


def mx_kscale(k):
    if not WIDE:
        return np.ones(k)
    levels = np.array([10, -10, 5, -5, 0])
    if k % 512:
        return np.exp2(np.random.permutation(np.resize(levels, k // 32))).repeat(32)
    a = np.empty((k // 512, 16))
    for p in range(k // 512):
        a[p, :8] = np.random.permutation(np.resize(levels, 8))
        for g in range(8):
            far = levels[np.abs(levels - a[p, g]) >= 10]
            a[p, g + 8] = far[np.random.randint(len(far))]
    return np.exp2(a.ravel()).repeat(32)


def f64(x):
    return np.asarray(x).astype(np.float64)


E2M1 = np.array([0.0, 0.5, 1.0, 1.5, 2.0, 3.0, 4.0, 6.0, -0.0, -0.5, -1.0, -1.5, -2.0, -3.0, -4.0, -6.0])


def pack_weight(w, fmt):
    k, n = w.shape
    w = f64(np.asarray(w, np.float32).astype(ml_dtypes.bfloat16)).reshape(k // 32, 32, n)
    amax = np.abs(w).max(1)
    if fmt == "e4m3":
        byte = np.frexp(amax)[1] - 1 + 127 - 7
    else:
        mant, ex = np.frexp(amax / 6.0)
        byte = np.where(mant > 0.5, ex, ex - 1) + 127
    byte = np.clip(np.where(amax > 0, byte, 1), 1, 254)
    scaled = (w * np.exp2(127.0 - byte)[:, None, :]).reshape(k, n).astype(np.float32)
    by_word = np.ascontiguousarray(scaled.reshape(k // 512, 128, 4, n).transpose(0, 1, 3, 2))
    if fmt == "e4m3":
        words = by_word.astype(ml_dtypes.float8_e4m3fn).view(np.uint8)
    else:
        c = by_word.astype(ml_dtypes.float4_e2m1fn).view(np.uint8) & 0xF
        words = (c[..., 0::2] | (c[..., 1::2] << 4)).reshape(k // 512, 128, 2 * n)
    return np.ascontiguousarray(words), np.ascontiguousarray(byte.astype(np.uint8).reshape(k // 512, 16, n))


def unpack_weight(words, scales, fmt):
    g, _, n = scales.shape
    words = np.ascontiguousarray(words).reshape(g, 128, n, -1)
    if fmt == "e4m3":
        vals = words.view(ml_dtypes.float8_e4m3fn).astype(np.float64)
    else:
        nib = np.empty((g, 128, n, 4), np.uint8)
        nib[..., 0::2] = words & 0xF
        nib[..., 1::2] = words >> 4
        vals = E2M1[nib]
    vals = vals * np.repeat(np.exp2(scales.astype(np.float64) - 127.0), 8, axis=1)[..., None]
    return vals.transpose(0, 1, 3, 2).reshape(g * 512, n)


def silu(v):
    return v / (1.0 + np.exp(-np.maximum(v, -700.0)))


O, K, M, T = 512, 1536, 2048, 512


def setup_inputs():
    n = np.random.standard_normal
    s = mx_kscale(K)[:, None]
    x = n((K, T)); x[:O] *= 6.0
    w = n((K, M)) / np.sqrt(K) / s; w[:O] /= 2.0
    p_w8 = pack_weight(w[:O], "e4m3")
    p_w4 = pack_weight(w[O:], "e2m1")
    return {
        "x": (x * s).astype(np.float32),
        "w8_words": p_w8[0],
        "w8_scales": p_w8[1],
        "w4_words": p_w4[0],
        "w4_scales": p_w4[1],
        "b": (0.3 * n(2048)).astype(np.float32),
    }


def reference(x, w8_words, w8_scales, w4_words, w4_scales, b):
    x_ = mxq(f64(x), 0, "e4m3")
    w8_ = unpack_weight(w8_words, w8_scales, "e4m3")
    w4_ = unpack_weight(w4_words, w4_scales, "e2m1")
    y = x_[:O].T @ w8_ + x_[O:].T @ w4_
    return silu(y + f64(b)[None, :])

@@ -1,0 +1,184 @@
+from contextlib import ExitStack
+
+import concourse.mybir as mybir
+from concourse.masks import make_identity
+
+K, N, T = 1536, 2048, 512
+FLOPS = 2 * K * N * T
+BYTES = 4 * K * T + 512 * N + 16 * N + 1024 * N // 2 + 32 * N + 4 * N + 4 * T * N
+
+F32 = mybir.dt.float32
+BF16 = mybir.dt.bfloat16
+I32 = mybir.dt.int32
+U32 = mybir.dt.uint32
+U8 = mybir.dt.uint8
+FP8X4 = mybir.dt.float8_e4m3fn_x4
+FP4X4 = mybir.dt.float4_e2m1fn_x4
+ADD = mybir.AluOpType.add
+SILU = mybir.ActivationFunctionType.Silu
+
+P = 128
+PACK = 4
+PASSES = 3
+NT = 512
+HALF = 1024
+VEC_COLS = 320
+
+
+def tile_mix_outl_tm_silu_kernel(tc, x, w8_words, w8_scales, w4_words, w4_scales, b, out):
+    nc = tc.nc
+    with ExitStack() as ctx:
+        keep = ctx.enter_context(tc.tile_pool(name="keep", bufs=1))
+        psum = ctx.enter_context(tc.psum_pool(name="psum", bufs=1))
+
+        ident = keep.tile([P, P], F32, name="ident")
+        make_identity(nc, ident[:])
+
+        x_raw = [keep.tile([P, PACK, T], F32, name=f"x_raw{g}", align_bytes=64) for g in range(PASSES)]
+        x_bf = [keep.tile([P, T, PACK], BF16, name=f"x_bf{g}", align_bytes=64) for g in range(PASSES)]
+        x_codes = [keep.tile([P, T], U32, name=f"x_codes{g}", align_bytes=64) for g in range(PASSES)]
+        x_sc = [keep.tile([P, T], U8, name=f"x_sc{g}", align_bytes=64) for g in range(PASSES)]
+        w8 = keep.tile([P, PACK * N], U8, name="w8", align_bytes=256)
+        w4 = [keep.tile([P, 2 * N], U8, name=f"w4_{a}", align_bytes=256) for a in range(2)]
+        w8_sc = keep.tile([P, N], U8, name="w8_sc", align_bytes=256)
+        w4_sc = keep.tile([P, 2, N], U8, name="w4_sc", align_bytes=256)
+        b_cols = keep.tile([P, 16], F32, name="b_cols")
+        bias = keep.tile([P, N], F32, name="bias", align_bytes=64)
+        one = keep.tile([P, 1], F32, name="one")
+        one_out = keep.tile([P, 1], F32, name="one_out")
+
+        with tc.manual_schedule():
+            nc.vector.memset(one[:], 0.0)
+            nc.scalar.dma_start(out=b_cols[:], in_=b.rearrange("(p c) -> p c", c=16))
+            nc.scalar.activation(out=one_out[:], in_=one[:], func=SILU)
+            nc.vector.memset(w8_sc[:].bitcast(I32), 0)
+            nc.vector.memset(w4_sc[:].rearrange("p a n -> p (a n)").bitcast(I32), 0)
+
+            def load_x(g):
+                nc.sync.dma_start(out=x_raw[g][:], in_=x[512 * g : 512 * (g + 1), :].rearrange("(p j) t -> p j t", j=PACK))
+
+            def load_w8(h):
+                c = slice(h * HALF * 4, (h + 1) * HALF * 4)
+                nc.sync.dma_start(
+                    out=w8[:, c].bitcast(I32),
+                    in_=w8_words[0].rearrange("p n i -> p (n i)")[:, c].bitcast(I32),
+                )
+
+            def load_w4(a, h):
+                c = slice(h * HALF * 2, (h + 1) * HALF * 2)
+                nc.sync.dma_start(out=w4[a][:, c].bitcast(I32), in_=w4_words[a][:, c].bitcast(I32))
+
+            load_x(0)
+            for q in range(4):
+                nc.sync.dma_start(
+                    out=w8_sc[32 * q + 4 : 32 * q + 8, :].bitcast(I32),
+                    in_=w8_scales[0][4 * q : 4 * q + 4, :].bitcast(I32),
+                )
+            load_w8(0)
+            load_x(1)
+            for q in range(4):
+                nc.sync.dma_start(
+                    out=w4_sc[32 * q : 32 * q + 4, :, :].bitcast(I32),
+                    in_=w4_scales[:, 4 * q : 4 * q + 4, :].rearrange("a r n -> r a n").bitcast(I32),
+                )
+            load_w4(0, 0)
+            load_x(2)
+            load_w4(1, 0)
+            load_w8(1)
+            load_w4(0, 1)
+            load_w4(1, 1)
+
+            def grouped(engine_copy, g, c0, c1):
+                engine_copy(
+                    out=x_bf[g][:, c0:c1, :].rearrange("p (c i) j -> p c j i", i=4),
+                    in_=x_raw[g][:, :, c0:c1].rearrange("p j (c i) -> p c j i", i=4),
+                )
+
+            def quantize(g, c0, c1):
+                nc.vector.quantize_mx(
+                    out=x_codes[g][:, c0:c1].bitcast(FP8X4),
+                    scales=x_sc[g][:, c0:c1],
+                    in_=x_bf[g][:, c0:c1, :].rearrange("p t j -> p (t j)"),
+                )
+
+            def prepare_x(g):
+                grouped(nc.vector.tensor_copy, g, 0, 128)
+                grouped(nc.scalar.copy, g, VEC_COLS, T)
+                grouped(nc.vector.tensor_copy, g, 128, 256)
+                grouped(nc.vector.tensor_copy, g, 256, VEC_COLS)
+                quantize(g, 0, 256)
+                quantize(g, 256, 512)
+
+            def product(bank, g, t, n, start, stop):
+                tc0 = slice(t * P, (t + 1) * P)
+                n0 = slice(n * NT, (n + 1) * NT)
+                if g == 0:
+                    rhs = w8[:, n * NT * 4 : (n + 1) * NT * 4].bitcast(FP8X4)
+                    rhs_scale = w8_sc[4:P, n0]
+                else:
+                    rhs = w4[g - 1][:, n * NT * 2 : (n + 1) * NT * 2].bitcast(FP4X4)
+                    rhs_scale = w4_sc[:, g - 1, n0]
+                nc.tensor.matmul_mx(
+                    out=bank[:],
+                    lhsT=x_codes[g][:, tc0].bitcast(FP8X4),
+                    lhsT_scale=x_sc[g][:, tc0],
+                    rhs=rhs,
+                    rhs_scale=rhs_scale,
+                    start=start,
+                    stop=stop,
+                )
+
+            prepare_x(0)
+
+            for j in range(4):
+                spread = psum.tile([P, NT], F32, name=f"spread{j}", tag=f"bank{4 + j}")
+                for c in range(4):
+                    nc.tensor.transpose(
+                        spread[:, c * P : (c + 1) * P],
+                        b_cols[:, 4 * j + c : 4 * j + c + 1].to_broadcast([P, P]),
+                        ident[:],
+                    )
+                nc.scalar.copy(
+                    out=bias[:].rearrange("p (i c) -> p i c", c=16)[:, :, 4 * j : 4 * j + 4],
+                    in_=spread[:].rearrange("p (c i) -> p i c", c=4),
+                )
+
+            banks = {}
+            for g in range(PASSES):
+                if g > 0:
+                    prepare_x(g)
+                for t in range(4):
+                    for n in range(2):
+                        if g == 0:
+                            banks[(t, n)] = psum.tile([P, NT], F32, name=f"acc{t}_{n}", tag=f"bank{2 * t + n}")
+                        product(banks[(t, n)], g, t, n, g == 0, g == PASSES - 1)
+
+            z = [keep.tile([P, HALF], F32, name=f"z{i}", align_bytes=64) for i in range(8)]
+            y = [keep.tile([P, HALF], F32, name=f"y{i}", align_bytes=64) for i in range(8)]
+
+            def finish(t, n):
+                i = 4 * (n // 2) + t
+                c = slice((n % 2) * NT, (n % 2 + 1) * NT)
+                nc.vector.tensor_tensor(out=z[i][:, c], in0=banks[(t, n)][:], in1=bias[:, n * NT : (n + 1) * NT], op=ADD)
+                nc.scalar.activation(out=y[i][:, c], in_=z[i][:, c], func=SILU)
+
+            def store(t, h, c0, c1):
+                nc.sync.dma_start(
+                    out=out[t * P : (t + 1) * P, h * HALF + c0 : h * HALF + c1],
+                    in_=y[4 * h + t][:, c0:c1],
+                )
+
+            for t in range(4):
+                finish(t, 0)
+                finish(t, 1)
+                store(t, 0, 0, HALF)
+            for t in range(4):
+                for n in (2, 3):
+                    banks[(t, n)] = psum.tile([P, NT], F32, name=f"acc{t}_{n}", tag=f"bank{2 * t + n % 2}")
+                    for g in range(PASSES):
+                        product(banks[(t, n)], g, t, n, g == 0, g == PASSES - 1)
+                    finish(t, n)
+                    if t == 3:
+                        store(t, 1, (n % 2) * NT, (n % 2 + 1) * NT)
+                if t < 3:
+                    store(t, 1, 0, HALF)

@@ -22,7 +22,7 @@ PACK = 4
 PASSES = 3
 NT = 512
 HALF = 1024
-VEC_COLS = 320
+VEC_COLS = 288
 
 
 def tile_mix_outl_tm_silu_kernel(tc, x, w8_words, w8_scales, w4_words, w4_scales, b, out):
@@ -68,21 +68,21 @@ def tile_mix_outl_tm_silu_kernel(tc, x, w8_words, w8_scales, w4_words, w4_scales
                 c = slice(h * HALF * 2, (h + 1) * HALF * 2)
                 nc.sync.dma_start(out=w4[a][:, c].bitcast(I32), in_=w4_words[a][:, c].bitcast(I32))
 
+            def load_scales(plane, first, rows):
+                for r in range(4):
+                    nc.sync.dma_start(
+                        out=plane[first + r : P : 32, :].bitcast(I32),
+                        in_=rows.rearrange("(q r) n -> r q n", r=4)[r].bitcast(I32),
+                    )
+
             load_x(0)
-            for q in range(4):
-                nc.sync.dma_start(
-                    out=w8_sc[32 * q + 4 : 32 * q + 8, :].bitcast(I32),
-                    in_=w8_scales[0][4 * q : 4 * q + 4, :].bitcast(I32),
-                )
+            load_scales(w8_sc[:], 4, w8_scales[0])
             load_w8(0)
             load_x(1)
-            for q in range(4):
-                nc.sync.dma_start(
-                    out=w4_sc[32 * q : 32 * q + 4, :, :].bitcast(I32),
-                    in_=w4_scales[:, 4 * q : 4 * q + 4, :].rearrange("a r n -> r a n").bitcast(I32),
-                )
+            load_scales(w4_sc[:, 0, :], 0, w4_scales[0])
             load_w4(0, 0)
             load_x(2)
+            load_scales(w4_sc[:, 1, :], 0, w4_scales[1])
             load_w4(1, 0)
             load_w8(1)
             load_w4(0, 1)
@@ -104,9 +104,9 @@ def tile_mix_outl_tm_silu_kernel(tc, x, w8_words, w8_scales, w4_words, w4_scales
             def prepare_x(g):
                 grouped(nc.vector.tensor_copy, g, 0, 128)
                 grouped(nc.scalar.copy, g, VEC_COLS, T)
-                grouped(nc.vector.tensor_copy, g, 128, 256)
-                grouped(nc.vector.tensor_copy, g, 256, VEC_COLS)
-                quantize(g, 0, 256)
+                grouped(nc.vector.tensor_copy, g, 128, VEC_COLS)
+                quantize(g, 0, 128)
+                quantize(g, 128, 256)
                 quantize(g, 256, 512)
 
             def product(bank, g, t, n, start, stop):
@@ -156,10 +156,10 @@ def tile_mix_outl_tm_silu_kernel(tc, x, w8_words, w8_scales, w4_words, w4_scales
             z = [keep.tile([P, HALF], F32, name=f"z{i}", align_bytes=64) for i in range(8)]
             y = [keep.tile([P, HALF], F32, name=f"y{i}", align_bytes=64) for i in range(8)]
 
-            def finish(t, n):
+            def finish(t, n, a, e):
                 i = 4 * (n // 2) + t
-                c = slice((n % 2) * NT, (n % 2 + 1) * NT)
-                nc.vector.tensor_tensor(out=z[i][:, c], in0=banks[(t, n)][:], in1=bias[:, n * NT : (n + 1) * NT], op=ADD)
+                c = slice((n % 2) * NT + a, (n % 2) * NT + e)
+                nc.vector.tensor_tensor(out=z[i][:, c], in0=banks[(t, n)][:, a:e], in1=bias[:, n * NT + a : n * NT + e], op=ADD)
                 nc.scalar.activation(out=y[i][:, c], in_=z[i][:, c], func=SILU)
 
             def store(t, h, c0, c1):
@@ -169,16 +169,25 @@ def tile_mix_outl_tm_silu_kernel(tc, x, w8_words, w8_scales, w4_words, w4_scales
                 )
 
             for t in range(4):
-                finish(t, 0)
-                finish(t, 1)
-                store(t, 0, 0, HALF)
+                for n in range(2):
+                    finish(t, n, 0, NT)
+                    if t == 0:
+                        store(t, 0, n * NT, (n + 1) * NT)
+                if t > 0:
+                    store(t, 0, 0, HALF)
             for t in range(4):
                 for n in (2, 3):
                     banks[(t, n)] = psum.tile([P, NT], F32, name=f"acc{t}_{n}", tag=f"bank{2 * t + n % 2}")
                     for g in range(PASSES):
                         product(banks[(t, n)], g, t, n, g == 0, g == PASSES - 1)
-                    finish(t, n)
-                    if t == 3:
-                        store(t, 1, (n % 2) * NT, (n % 2 + 1) * NT)
+                    if t < 3:
+                        finish(t, n, 0, NT)
+                    elif n == 2:
+                        finish(t, n, 0, NT)
+                        store(t, 1, 0, NT)
+                    else:
+                        for a in (0, NT // 2):
+                            finish(t, n, a, a + NT // 2)
+                            store(t, 1, NT + a, NT + a + NT // 2)
                 if t < 3:
                     store(t, 1, 0, HALF)

@@ -41,7 +41,7 @@ def tile_mix_outl_tm_silu_kernel(tc, x, w8_words, w8_scales, w4_words, w4_scales
         w8 = keep.tile([P, PACK * N], U8, name="w8", align_bytes=256)
         w4 = [keep.tile([P, 2 * N], U8, name=f"w4_{a}", align_bytes=256) for a in range(2)]
         w8_sc = keep.tile([P, N], U8, name="w8_sc", align_bytes=256)
-        w4_sc = keep.tile([P, 2, N], U8, name="w4_sc", align_bytes=256)
+        w4_sc = [keep.tile([P, N], U8, name=f"w4_sc{a}", align_bytes=256) for a in range(2)]
         b_cols = keep.tile([P, 16], F32, name="b_cols")
         bias = keep.tile([P, N], F32, name="bias", align_bytes=64)
         one = keep.tile([P, 1], F32, name="one")
@@ -52,7 +52,8 @@ def tile_mix_outl_tm_silu_kernel(tc, x, w8_words, w8_scales, w4_words, w4_scales
             nc.scalar.dma_start(out=b_cols[:], in_=b.rearrange("(p c) -> p c", c=16))
             nc.scalar.activation(out=one_out[:], in_=one[:], func=SILU)
             nc.vector.memset(w8_sc[:].bitcast(I32), 0)
-            nc.vector.memset(w4_sc[:].rearrange("p a n -> p (a n)").bitcast(I32), 0)
+            for a in range(2):
+                nc.vector.memset(w4_sc[a][:].bitcast(I32), 0)
 
             def load_x(g):
                 nc.sync.dma_start(out=x_raw[g][:], in_=x[512 * g : 512 * (g + 1), :].rearrange("(p j) t -> p j t", j=PACK))
@@ -79,10 +80,10 @@ def tile_mix_outl_tm_silu_kernel(tc, x, w8_words, w8_scales, w4_words, w4_scales
             load_scales(w8_sc[:], 4, w8_scales[0])
             load_w8(0)
             load_x(1)
-            load_scales(w4_sc[:, 0, :], 0, w4_scales[0])
+            load_scales(w4_sc[0][:], 0, w4_scales[0])
             load_w4(0, 0)
             load_x(2)
-            load_scales(w4_sc[:, 1, :], 0, w4_scales[1])
+            load_scales(w4_sc[1][:], 0, w4_scales[1])
             load_w4(1, 0)
             load_w8(1)
             load_w4(0, 1)
@@ -117,7 +118,7 @@ def tile_mix_outl_tm_silu_kernel(tc, x, w8_words, w8_scales, w4_words, w4_scales
                     rhs_scale = w8_sc[4:P, n0]
                 else:
                     rhs = w4[g - 1][:, n * NT * 2 : (n + 1) * NT * 2].bitcast(FP4X4)
-                    rhs_scale = w4_sc[:, g - 1, n0]
+                    rhs_scale = w4_sc[g - 1][:, n0]
                 nc.tensor.matmul_mx(
                     out=bank[:],
                     lhsT=x_codes[g][:, tc0].bitcast(FP8X4),

from contextlib import ExitStack

import concourse.mybir as mybir
from concourse.masks import make_identity

K, N, T = 1536, 2048, 512
FLOPS = 2 * K * N * T
BYTES = 4 * K * T + 512 * N + 16 * N + 1024 * N // 2 + 32 * N + 4 * N + 4 * T * N

F32 = mybir.dt.float32
BF16 = mybir.dt.bfloat16
I32 = mybir.dt.int32
U32 = mybir.dt.uint32
U8 = mybir.dt.uint8
FP8X4 = mybir.dt.float8_e4m3fn_x4
FP4X4 = mybir.dt.float4_e2m1fn_x4
ADD = mybir.AluOpType.add
SILU = mybir.ActivationFunctionType.Silu

P = 128
PACK = 4
PASSES = 3
NT = 512
HALF = 1024
VEC_COLS = 288


def tile_mix_outl_tm_silu_kernel(tc, x, w8_words, w8_scales, w4_words, w4_scales, b, out):
    nc = tc.nc
    with ExitStack() as ctx:
        keep = ctx.enter_context(tc.tile_pool(name="keep", bufs=1))
        psum = ctx.enter_context(tc.psum_pool(name="psum", bufs=1))

        ident = keep.tile([P, P], F32, name="ident")
        make_identity(nc, ident[:])

        x_raw = [keep.tile([P, PACK, T], F32, name=f"x_raw{g}", align_bytes=64) for g in range(PASSES)]
        x_bf = [keep.tile([P, T, PACK], BF16, name=f"x_bf{g}", align_bytes=64) for g in range(PASSES)]
        x_codes = [keep.tile([P, T], U32, name=f"x_codes{g}", align_bytes=64) for g in range(PASSES)]
        x_sc = [keep.tile([P, T], U8, name=f"x_sc{g}", align_bytes=64) for g in range(PASSES)]
        w8 = keep.tile([P, PACK * N], U8, name="w8", align_bytes=256)
        w4 = [keep.tile([P, 2 * N], U8, name=f"w4_{a}", align_bytes=256) for a in range(2)]
        w8_sc = keep.tile([P, N], U8, name="w8_sc", align_bytes=256)
        w4_sc = [keep.tile([P, N], U8, name=f"w4_sc{a}", align_bytes=256) for a in range(2)]
        b_cols = keep.tile([P, 16], F32, name="b_cols")
        bias = keep.tile([P, N], F32, name="bias", align_bytes=64)
        one = keep.tile([P, 1], F32, name="one")
        one_out = keep.tile([P, 1], F32, name="one_out")

        with tc.manual_schedule():
            nc.vector.memset(one[:], 0.0)
            nc.scalar.dma_start(out=b_cols[:], in_=b.rearrange("(p c) -> p c", c=16))
            nc.scalar.activation(out=one_out[:], in_=one[:], func=SILU)
            nc.vector.memset(w8_sc[:].bitcast(I32), 0)
            for a in range(2):
                nc.vector.memset(w4_sc[a][:].bitcast(I32), 0)

            def load_x(g):
                nc.sync.dma_start(out=x_raw[g][:], in_=x[512 * g : 512 * (g + 1), :].rearrange("(p j) t -> p j t", j=PACK))

            def load_w8(h):
                c = slice(h * HALF * 4, (h + 1) * HALF * 4)
                nc.sync.dma_start(
                    out=w8[:, c].bitcast(I32),
                    in_=w8_words[0].rearrange("p n i -> p (n i)")[:, c].bitcast(I32),
                )

            def load_w4(a, h):
                c = slice(h * HALF * 2, (h + 1) * HALF * 2)
                nc.sync.dma_start(out=w4[a][:, c].bitcast(I32), in_=w4_words[a][:, c].bitcast(I32))

            def load_scales(plane, first, rows):
                for r in range(4):
                    nc.sync.dma_start(
                        out=plane[first + r : P : 32, :].bitcast(I32),
                        in_=rows.rearrange("(q r) n -> r q n", r=4)[r].bitcast(I32),
                    )

            load_x(0)
            load_scales(w8_sc[:], 4, w8_scales[0])
            load_w8(0)
            load_x(1)
            load_scales(w4_sc[0][:], 0, w4_scales[0])
            load_w4(0, 0)
            load_x(2)
            load_scales(w4_sc[1][:], 0, w4_scales[1])
            load_w4(1, 0)
            load_w8(1)
            load_w4(0, 1)
            load_w4(1, 1)

            def grouped(engine_copy, g, c0, c1):
                engine_copy(
                    out=x_bf[g][:, c0:c1, :].rearrange("p (c i) j -> p c j i", i=4),
                    in_=x_raw[g][:, :, c0:c1].rearrange("p j (c i) -> p c j i", i=4),
                )

            def quantize(g, c0, c1):
                nc.vector.quantize_mx(
                    out=x_codes[g][:, c0:c1].bitcast(FP8X4),
                    scales=x_sc[g][:, c0:c1],
                    in_=x_bf[g][:, c0:c1, :].rearrange("p t j -> p (t j)"),
                )

            def prepare_x(g):
                grouped(nc.vector.tensor_copy, g, 0, 128)
                grouped(nc.scalar.copy, g, VEC_COLS, T)
                grouped(nc.vector.tensor_copy, g, 128, VEC_COLS)
                quantize(g, 0, 128)
                quantize(g, 128, 256)
                quantize(g, 256, 512)

            def product(bank, g, t, n, start, stop):
                tc0 = slice(t * P, (t + 1) * P)
                n0 = slice(n * NT, (n + 1) * NT)
                if g == 0:
                    rhs = w8[:, n * NT * 4 : (n + 1) * NT * 4].bitcast(FP8X4)
                    rhs_scale = w8_sc[4:P, n0]
                else:
                    rhs = w4[g - 1][:, n * NT * 2 : (n + 1) * NT * 2].bitcast(FP4X4)
                    rhs_scale = w4_sc[g - 1][:, n0]
                nc.tensor.matmul_mx(
                    out=bank[:],
                    lhsT=x_codes[g][:, tc0].bitcast(FP8X4),
                    lhsT_scale=x_sc[g][:, tc0],
                    rhs=rhs,
                    rhs_scale=rhs_scale,
                    start=start,
                    stop=stop,
                )

            prepare_x(0)

            for j in range(4):
                spread = psum.tile([P, NT], F32, name=f"spread{j}", tag=f"bank{4 + j}")
                for c in range(4):
                    nc.tensor.transpose(
                        spread[:, c * P : (c + 1) * P],
                        b_cols[:, 4 * j + c : 4 * j + c + 1].to_broadcast([P, P]),
                        ident[:],
                    )
                nc.scalar.copy(
                    out=bias[:].rearrange("p (i c) -> p i c", c=16)[:, :, 4 * j : 4 * j + 4],
                    in_=spread[:].rearrange("p (c i) -> p i c", c=4),
                )

            banks = {}
            for g in range(PASSES):
                if g > 0:
                    prepare_x(g)
                for t in range(4):
                    for n in range(2):
                        if g == 0:
                            banks[(t, n)] = psum.tile([P, NT], F32, name=f"acc{t}_{n}", tag=f"bank{2 * t + n}")
                        product(banks[(t, n)], g, t, n, g == 0, g == PASSES - 1)

            z = [keep.tile([P, HALF], F32, name=f"z{i}", align_bytes=64) for i in range(8)]
            y = [keep.tile([P, HALF], F32, name=f"y{i}", align_bytes=64) for i in range(8)]

            def finish(t, n, a, e):
                i = 4 * (n // 2) + t
                c = slice((n % 2) * NT + a, (n % 2) * NT + e)
                nc.vector.tensor_tensor(out=z[i][:, c], in0=banks[(t, n)][:, a:e], in1=bias[:, n * NT + a : n * NT + e], op=ADD)
                nc.scalar.activation(out=y[i][:, c], in_=z[i][:, c], func=SILU)

            def store(t, h, c0, c1):
                nc.sync.dma_start(
                    out=out[t * P : (t + 1) * P, h * HALF + c0 : h * HALF + c1],
                    in_=y[4 * h + t][:, c0:c1],
                )

            for t in range(4):
                for n in range(2):
                    finish(t, n, 0, NT)
                    if t == 0:
                        store(t, 0, n * NT, (n + 1) * NT)
                if t > 0:
                    store(t, 0, 0, HALF)
            for t in range(4):
                for n in (2, 3):
                    banks[(t, n)] = psum.tile([P, NT], F32, name=f"acc{t}_{n}", tag=f"bank{2 * t + n % 2}")
                    for g in range(PASSES):
                        product(banks[(t, n)], g, t, n, g == 0, g == PASSES - 1)
                    if t < 3:
                        finish(t, n, 0, NT)
                    elif n == 2:
                        finish(t, n, 0, NT)
                        store(t, 1, 0, NT)
                    else:
                        for a in (0, NT // 2):
                            finish(t, n, a, a + NT // 2)
                            store(t, 1, NT + a, NT + a + NT // 2)
                if t < 3:
                    store(t, 1, 0, HALF)
